import numpy as np
import ml_dtypes

BF16 = ml_dtypes.bfloat16


def bf(x):
    return np.asarray(x, np.float32).astype(BF16)


def f32(x):
    return np.asarray(x, np.float32)


def f64(x):
    return np.asarray(x).astype(np.float64)


def striped(idx):
    return np.tile(idx.reshape(-1, 16).T, (8, 1))


S, K, M, N, E, Q = 1024, 128, 256, 2048, 4, 512


def gelu_tanh(v):
    return 0.5 * v * (1.0 + np.tanh(np.sqrt(2.0 / np.pi) * (v + 0.044715 * v**3)))


def two_experts():
    first = np.random.permutation(S).reshape(E, S // E)
    return np.concatenate([np.random.permutation(np.concatenate([first[e], first[(e + 1) % E]])) for e in range(E)])


def setup_inputs():
    return {"table": bf(np.random.standard_normal((S, K))), "w": bf(np.random.standard_normal((E, K, M)) / np.sqrt(K)), "b": f32(0.5 * np.random.standard_normal((M, 1))), "offs": striped(two_experts())}


def reference(table, w, b, offs):
    idx = offs[:16].T.reshape(-1)
    x = f64(table)[idx].T
    y = np.concatenate([f64(w)[e].T @ x[:, e * Q : (e + 1) * Q] for e in range(E)], axis=1)
    return gelu_tanh(y + f64(b))

@@ -1,0 +1,56 @@
+import concourse.mybir as mybir
+from concourse.masks import make_identity
+
+BF16, F32, U16 = mybir.dt.bfloat16, mybir.dt.float32, mybir.dt.uint16
+GELU = mybir.ActivationFunctionType.Gelu_apprx_tanh
+
+P = 128
+S, K, M, N, E = 1024, 128, 256, 2048, 4
+Q = N // E
+TOKEN_BLOCKS = S // P
+HALF = TOKEN_BLOCKS // 2
+OUT_BLOCKS = M // P
+
+FLOPS = 2 * K * M * N
+
+
+def tile_gather_matmul_kernel(tc, table, w, b, offs, out):
+    nc = tc.nc
+    with (
+        tc.tile_pool(name="held", bufs=1) as held,
+        tc.tile_pool(name="results", bufs=E * OUT_BLOCKS) as results,
+        tc.psum_pool(name="flips", bufs=2) as flips,
+        tc.psum_pool(name="products", bufs=6) as products,
+    ):
+        offsets = held.tile([P, N // 16], U16, name="offsets")
+        nc.sync.dma_start(offsets[:], offs)
+
+        token_rows = table.rearrange("(h a p) k -> h p a k", h=2, p=P)
+        rows = [held.tile([P, HALF, K], BF16, name="rows%d" % h) for h in range(2)]
+        nc.sync.dma_start(rows[0][:], token_rows[0])
+        nc.scalar.dma_start(rows[1][:], token_rows[1])
+
+        identity = held.tile([P, P], BF16, name="identity")
+        make_identity(nc, identity[:])
+
+        weights = held.tile([P, E, M], BF16, name="weights")
+        nc.gpsimd.dma_start(weights[:], w.rearrange("e k m -> k e m"))
+
+        bias = held.tile([P, OUT_BLOCKS], F32, name="bias")
+        nc.scalar.dma_start(bias[:], b.rearrange("(a p) o -> p (a o)", p=P))
+
+        tokens = held.tile([P, S], BF16, name="tokens")
+        for h in range(2):
+            flipped = flips.tile([P, HALF * P], BF16, name="flipped")
+            for a in range(HALF):
+                nc.tensor.transpose(flipped[:, a * P : (a + 1) * P], rows[h][:, a, :], identity[:])
+            nc.vector.tensor_copy(tokens[:, h * HALF * P : (h + 1) * HALF * P], flipped[:])
+
+        for e in range(E):
+            picked = tokens[:].indirect(offsets[:, e * (Q // 16) : (e + 1) * (Q // 16)])
+            for a in range(OUT_BLOCKS):
+                product = products.tile([P, Q], F32, name="product")
+                nc.tensor.matmul(product[:], weights[:, e, a * P : (a + 1) * P], picked, start=True, stop=True)
+                result = results.tile([P, Q], F32, name="result")
+                nc.scalar.activation(result[:], product[:], GELU, bias=bias[:, a : a + 1])
+                nc.sync.dma_start(out[a * P : (a + 1) * P, e * Q : (e + 1) * Q], result[:])

@@ -7,8 +7,8 @@ GELU = mybir.ActivationFunctionType.Gelu_apprx_tanh
 P = 128
 S, K, M, N, E = 1024, 128, 256, 2048, 4
 Q = N // E
-TOKEN_BLOCKS = S // P
-HALF = TOKEN_BLOCKS // 2
+CHUNKS = 4
+BLOCKS = S // P // CHUNKS
 OUT_BLOCKS = M // P
 
 FLOPS = 2 * K * M * N
@@ -25,26 +25,32 @@ def tile_gather_matmul_kernel(tc, table, w, b, offs, out):
         offsets = held.tile([P, N // 16], U16, name="offsets")
         nc.sync.dma_start(offsets[:], offs)
 
-        token_rows = table.rearrange("(h a p) k -> h p a k", h=2, p=P)
-        rows = [held.tile([P, HALF, K], BF16, name="rows%d" % h) for h in range(2)]
-        nc.sync.dma_start(rows[0][:], token_rows[0])
-        nc.scalar.dma_start(rows[1][:], token_rows[1])
-
-        identity = held.tile([P, P], BF16, name="identity")
-        make_identity(nc, identity[:])
+        token_rows = table.rearrange("(c a p) k -> c p a k", c=CHUNKS, p=P)
+        rows = [held.tile([P, BLOCKS, K], BF16, name="rows%d" % c) for c in range(CHUNKS)]
+        for c in range(CHUNKS):
+            queue = nc.sync if c % 2 == 0 else nc.scalar
+            queue.dma_start(rows[c][:], token_rows[c])
 
         weights = held.tile([P, E, M], BF16, name="weights")
-        nc.gpsimd.dma_start(weights[:], w.rearrange("e k m -> k e m"))
+        nc.sync.dma_start(weights[:], w.rearrange("e k m -> k e m"))
 
         bias = held.tile([P, OUT_BLOCKS], F32, name="bias")
         nc.scalar.dma_start(bias[:], b.rearrange("(a p) o -> p (a o)", p=P))
 
+        zero = held.tile([P, 1], F32, name="zero")
+        nc.vector.memset(zero[:], 0.0)
+        gelu_of_zero = held.tile([P, 1], F32, name="gelu_of_zero")
+        nc.scalar.activation(gelu_of_zero[:], zero[:], GELU)
+
+        identity = held.tile([P, P], BF16, name="identity")
+        make_identity(nc, identity[:])
+
         tokens = held.tile([P, S], BF16, name="tokens")
-        for h in range(2):
-            flipped = flips.tile([P, HALF * P], BF16, name="flipped")
-            for a in range(HALF):
-                nc.tensor.transpose(flipped[:, a * P : (a + 1) * P], rows[h][:, a, :], identity[:])
-            nc.vector.tensor_copy(tokens[:, h * HALF * P : (h + 1) * HALF * P], flipped[:])
+        for c in range(CHUNKS):
+            flipped = flips.tile([P, BLOCKS * P], BF16, name="flipped")
+            for a in range(BLOCKS):
+                nc.tensor.transpose(flipped[:, a * P : (a + 1) * P], rows[c][:, a, :], identity[:])
+            nc.vector.tensor_copy(tokens[:, c * BLOCKS * P : (c + 1) * BLOCKS * P], flipped[:])
 
         for e in range(E):
             picked = tokens[:].indirect(offsets[:, e * (Q // 16) : (e + 1) * (Q // 16)])

@@ -10,6 +10,7 @@ Q = N // E
 CHUNKS = 4
 BLOCKS = S // P // CHUNKS
 OUT_BLOCKS = M // P
+WARM_UP = 4
 
 FLOPS = 2 * K * M * N
 
@@ -20,7 +21,8 @@ def tile_gather_matmul_kernel(tc, table, w, b, offs, out):
         tc.tile_pool(name="held", bufs=1) as held,
         tc.tile_pool(name="results", bufs=E * OUT_BLOCKS) as results,
         tc.psum_pool(name="flips", bufs=2) as flips,
-        tc.psum_pool(name="products", bufs=6) as products,
+        tc.psum_pool(name="unread", bufs=1) as unread,
+        tc.psum_pool(name="products", bufs=5) as products,
     ):
         offsets = held.tile([P, N // 16], U16, name="offsets")
         nc.sync.dma_start(offsets[:], offs)
@@ -45,12 +47,21 @@ def tile_gather_matmul_kernel(tc, table, w, b, offs, out):
         identity = held.tile([P, P], BF16, name="identity")
         make_identity(nc, identity[:])
 
+        zeros = held.tile([P, Q], BF16, name="zeros")
+        nc.vector.memset(zeros[:], 0.0)
+        warmth = unread.tile([P, Q], F32, name="warmth")
+        for i in range(WARM_UP):
+            nc.tensor.matmul(warmth[:], zeros[:, :P], zeros[:], start=True, stop=True)
+
         tokens = held.tile([P, S], BF16, name="tokens")
         for c in range(CHUNKS):
             flipped = flips.tile([P, BLOCKS * P], BF16, name="flipped")
             for a in range(BLOCKS):
                 nc.tensor.transpose(flipped[:, a * P : (a + 1) * P], rows[c][:, a, :], identity[:])
             nc.vector.tensor_copy(tokens[:, c * BLOCKS * P : (c + 1) * BLOCKS * P], flipped[:])
+            nc.tensor.matmul(
+                warmth[:, : BLOCKS * K], identity[:], rows[c][:].rearrange("p a k -> p (a k)"), start=True, stop=True
+            )
 
         for e in range(E):
             picked = tokens[:].indirect(offsets[:, e * (Q // 16) : (e + 1) * (Q // 16)])

@@ -24,8 +24,6 @@ def tile_gather_matmul_kernel(tc, table, w, b, offs, out):
         tc.psum_pool(name="unread", bufs=1) as unread,
         tc.psum_pool(name="products", bufs=5) as products,
     ):
-        offsets = held.tile([P, N // 16], U16, name="offsets")
-        nc.sync.dma_start(offsets[:], offs)
 
         token_rows = table.rearrange("(c a p) k -> c p a k", c=CHUNKS, p=P)
         rows = [held.tile([P, BLOCKS, K], BF16, name="rows%d" % c) for c in range(CHUNKS)]
@@ -33,8 +31,15 @@ def tile_gather_matmul_kernel(tc, table, w, b, offs, out):
             queue = nc.sync if c % 2 == 0 else nc.scalar
             queue.dma_start(rows[c][:], token_rows[c])
 
-        weights = held.tile([P, E, M], BF16, name="weights")
-        nc.sync.dma_start(weights[:], w.rearrange("e k m -> k e m"))
+        offsets = held.tile([P, N // 16], U16, name="offsets")
+        nc.sync.dma_start(offsets[:], offs)
+
+        features_first = w.rearrange("e k m -> k e m")
+        first_weights = held.tile([P, 1, M], BF16, name="first_weights")
+        nc.scalar.dma_start(first_weights[:], features_first[:, :1, :])
+        other_weights = held.tile([P, E - 1, M], BF16, name="other_weights")
+        nc.sync.dma_start(other_weights[:], features_first[:, 1:, :])
+        weights = [first_weights[:, 0, :]] + [other_weights[:, e, :] for e in range(E - 1)]
 
         bias = held.tile([P, OUT_BLOCKS], F32, name="bias")
         nc.scalar.dma_start(bias[:], b.rearrange("(a p) o -> p (a o)", p=P))
@@ -67,7 +72,7 @@ def tile_gather_matmul_kernel(tc, table, w, b, offs, out):
             picked = tokens[:].indirect(offsets[:, e * (Q // 16) : (e + 1) * (Q // 16)])
             for a in range(OUT_BLOCKS):
                 product = products.tile([P, Q], F32, name="product")
-                nc.tensor.matmul(product[:], weights[:, e, a * P : (a + 1) * P], picked, start=True, stop=True)
+                nc.tensor.matmul(product[:], weights[e][:, a * P : (a + 1) * P], picked, start=True, stop=True)
                 result = results.tile([P, Q], F32, name="result")
                 nc.scalar.activation(result[:], product[:], GELU, bias=bias[:, a : a + 1])
                 nc.sync.dma_start(out[a * P : (a + 1) * P, e * Q : (e + 1) * Q], result[:])

@@ -7,10 +7,11 @@ GELU = mybir.ActivationFunctionType.Gelu_apprx_tanh
 P = 128
 S, K, M, N, E = 1024, 128, 256, 2048, 4
 Q = N // E
-CHUNKS = 4
-BLOCKS = S // P // CHUNKS
+HALVES = 2
+BLOCKS = S // P // HALVES
+PAIR = 2
 OUT_BLOCKS = M // P
-WARM_UP = 4
+WARM_UP = 8
 
 FLOPS = 2 * K * M * N
 
@@ -20,16 +21,15 @@ def tile_gather_matmul_kernel(tc, table, w, b, offs, out):
     with (
         tc.tile_pool(name="held", bufs=1) as held,
         tc.tile_pool(name="results", bufs=E * OUT_BLOCKS) as results,
-        tc.psum_pool(name="flips", bufs=2) as flips,
+        tc.psum_pool(name="flips", bufs=3) as flips,
         tc.psum_pool(name="unread", bufs=1) as unread,
-        tc.psum_pool(name="products", bufs=5) as products,
+        tc.psum_pool(name="products", bufs=4) as products,
     ):
 
-        token_rows = table.rearrange("(c a p) k -> c p a k", c=CHUNKS, p=P)
-        rows = [held.tile([P, BLOCKS, K], BF16, name="rows%d" % c) for c in range(CHUNKS)]
-        for c in range(CHUNKS):
-            queue = nc.sync if c % 2 == 0 else nc.scalar
-            queue.dma_start(rows[c][:], token_rows[c])
+        token_rows = table.rearrange("(h a p) k -> h p a k", h=HALVES, p=P)
+        rows = [held.tile([P, BLOCKS, K], BF16, name="rows%d" % h) for h in range(HALVES)]
+        nc.sync.dma_start(rows[0][:], token_rows[0])
+        nc.scalar.dma_start(rows[1][:], token_rows[1])
 
         offsets = held.tile([P, N // 16], U16, name="offsets")
         nc.sync.dma_start(offsets[:], offs)
@@ -37,12 +37,13 @@ def tile_gather_matmul_kernel(tc, table, w, b, offs, out):
         features_first = w.rearrange("e k m -> k e m")
         first_weights = held.tile([P, 1, M], BF16, name="first_weights")
         nc.scalar.dma_start(first_weights[:], features_first[:, :1, :])
+
+        bias = held.tile([P, OUT_BLOCKS], F32, name="bias")
+        nc.sync.dma_start(bias[:], b.rearrange("(a p) o -> p (a o)", p=P))
+
         other_weights = held.tile([P, E - 1, M], BF16, name="other_weights")
         nc.sync.dma_start(other_weights[:], features_first[:, 1:, :])
         weights = [first_weights[:, 0, :]] + [other_weights[:, e, :] for e in range(E - 1)]
-
-        bias = held.tile([P, OUT_BLOCKS], F32, name="bias")
-        nc.scalar.dma_start(bias[:], b.rearrange("(a p) o -> p (a o)", p=P))
 
         zero = held.tile([P, 1], F32, name="zero")
         nc.vector.memset(zero[:], 0.0)
@@ -52,21 +53,22 @@ def tile_gather_matmul_kernel(tc, table, w, b, offs, out):
         identity = held.tile([P, P], BF16, name="identity")
         make_identity(nc, identity[:])
 
-        zeros = held.tile([P, Q], BF16, name="zeros")
-        nc.vector.memset(zeros[:], 0.0)
-        warmth = unread.tile([P, Q], F32, name="warmth")
+        warmth = unread.tile([P, P], F32, name="warmth")
         for i in range(WARM_UP):
-            nc.tensor.matmul(warmth[:], zeros[:, :P], zeros[:], start=True, stop=True)
+            nc.tensor.matmul(warmth[:], identity[:], identity[:], start=True, stop=True)
 
         tokens = held.tile([P, S], BF16, name="tokens")
-        for c in range(CHUNKS):
-            flipped = flips.tile([P, BLOCKS * P], BF16, name="flipped")
-            for a in range(BLOCKS):
-                nc.tensor.transpose(flipped[:, a * P : (a + 1) * P], rows[c][:, a, :], identity[:])
-            nc.vector.tensor_copy(tokens[:, c * BLOCKS * P : (c + 1) * BLOCKS * P], flipped[:])
-            nc.tensor.matmul(
-                warmth[:, : BLOCKS * K], identity[:], rows[c][:].rearrange("p a k -> p (a k)"), start=True, stop=True
-            )
+        for h in range(HALVES):
+            for pair in range(BLOCKS // PAIR):
+                flipped = flips.tile([P, PAIR * P], BF16, name="flipped")
+                for i in range(PAIR):
+                    nc.tensor.transpose(flipped[:, i * P : (i + 1) * P], rows[h][:, pair * PAIR + i, :], identity[:])
+                first_token = (h * BLOCKS + pair * PAIR) * P
+                window_part = tokens[:, first_token : first_token + PAIR * P]
+                if pair % 2 == 0:
+                    nc.vector.tensor_copy(window_part, flipped[:])
+                else:
+                    nc.scalar.copy(window_part, flipped[:])
 
         for e in range(E):
             picked = tokens[:].indirect(offsets[:, e * (Q // 16) : (e + 1) * (Q // 16)])

@@ -7,9 +7,8 @@ GELU = mybir.ActivationFunctionType.Gelu_apprx_tanh
 P = 128
 S, K, M, N, E = 1024, 128, 256, 2048, 4
 Q = N // E
-HALVES = 2
-BLOCKS = S // P // HALVES
-PAIR = 2
+CHUNKS = 4
+BLOCKS = S // P // CHUNKS
 OUT_BLOCKS = M // P
 WARM_UP = 8
 
@@ -26,10 +25,11 @@ def tile_gather_matmul_kernel(tc, table, w, b, offs, out):
         tc.psum_pool(name="products", bufs=4) as products,
     ):
 
-        token_rows = table.rearrange("(h a p) k -> h p a k", h=HALVES, p=P)
-        rows = [held.tile([P, BLOCKS, K], BF16, name="rows%d" % h) for h in range(HALVES)]
-        nc.sync.dma_start(rows[0][:], token_rows[0])
-        nc.scalar.dma_start(rows[1][:], token_rows[1])
+        token_rows = table.rearrange("(c a p) k -> c p a k", c=CHUNKS, p=P)
+        rows = [held.tile([P, BLOCKS, K], BF16, name="rows%d" % c) for c in range(CHUNKS)]
+        for c in range(CHUNKS):
+            queue = nc.sync if c % 2 == 0 else nc.scalar
+            queue.dma_start(rows[c][:], token_rows[c])
 
         offsets = held.tile([P, N // 16], U16, name="offsets")
         nc.sync.dma_start(offsets[:], offs)
@@ -58,17 +58,15 @@ def tile_gather_matmul_kernel(tc, table, w, b, offs, out):
             nc.tensor.matmul(warmth[:], identity[:], identity[:], start=True, stop=True)
 
         tokens = held.tile([P, S], BF16, name="tokens")
-        for h in range(HALVES):
-            for pair in range(BLOCKS // PAIR):
-                flipped = flips.tile([P, PAIR * P], BF16, name="flipped")
-                for i in range(PAIR):
-                    nc.tensor.transpose(flipped[:, i * P : (i + 1) * P], rows[h][:, pair * PAIR + i, :], identity[:])
-                first_token = (h * BLOCKS + pair * PAIR) * P
-                window_part = tokens[:, first_token : first_token + PAIR * P]
-                if pair % 2 == 0:
-                    nc.vector.tensor_copy(window_part, flipped[:])
-                else:
-                    nc.scalar.copy(window_part, flipped[:])
+        for c in range(CHUNKS):
+            flipped = flips.tile([P, BLOCKS * P], BF16, name="flipped")
+            for a in range(BLOCKS):
+                nc.tensor.transpose(flipped[:, a * P : (a + 1) * P], rows[c][:, a, :], identity[:])
+            window_part = tokens[:, c * BLOCKS * P : (c + 1) * BLOCKS * P]
+            if c % 2 == 0:
+                nc.vector.tensor_copy(window_part, flipped[:])
+            else:
+                nc.scalar.copy(window_part, flipped[:])
 
         for e in range(E):
             picked = tokens[:].indirect(offsets[:, e * (Q // 16) : (e + 1) * (Q // 16)])

@@ -10,7 +10,6 @@ Q = N // E
 CHUNKS = 4
 BLOCKS = S // P // CHUNKS
 OUT_BLOCKS = M // P
-WARM_UP = 8
 
 FLOPS = 2 * K * M * N
 
@@ -21,7 +20,6 @@ def tile_gather_matmul_kernel(tc, table, w, b, offs, out):
         tc.tile_pool(name="held", bufs=1) as held,
         tc.tile_pool(name="results", bufs=E * OUT_BLOCKS) as results,
         tc.psum_pool(name="flips", bufs=3) as flips,
-        tc.psum_pool(name="unread", bufs=1) as unread,
         tc.psum_pool(name="products", bufs=4) as products,
     ):
 
@@ -52,10 +50,6 @@ def tile_gather_matmul_kernel(tc, table, w, b, offs, out):
 
         identity = held.tile([P, P], BF16, name="identity")
         make_identity(nc, identity[:])
-
-        warmth = unread.tile([P, P], F32, name="warmth")
-        for i in range(WARM_UP):
-            nc.tensor.matmul(warmth[:], identity[:], identity[:], start=True, stop=True)
 
         tokens = held.tile([P, S], BF16, name="tokens")
         for c in range(CHUNKS):

@@ -26,15 +26,14 @@ def tile_gather_matmul_kernel(tc, table, w, b, offs, out):
         token_rows = table.rearrange("(c a p) k -> c p a k", c=CHUNKS, p=P)
         rows = [held.tile([P, BLOCKS, K], BF16, name="rows%d" % c) for c in range(CHUNKS)]
         for c in range(CHUNKS):
-            queue = nc.sync if c % 2 == 0 else nc.scalar
-            queue.dma_start(rows[c][:], token_rows[c])
+            nc.sync.dma_start(rows[c][:], token_rows[c])
 
         offsets = held.tile([P, N // 16], U16, name="offsets")
         nc.sync.dma_start(offsets[:], offs)
 
         features_first = w.rearrange("e k m -> k e m")
         first_weights = held.tile([P, 1, M], BF16, name="first_weights")
-        nc.scalar.dma_start(first_weights[:], features_first[:, :1, :])
+        nc.sync.dma_start(first_weights[:], features_first[:, :1, :])
 
         bias = held.tile([P, OUT_BLOCKS], F32, name="bias")
         nc.sync.dma_start(bias[:], b.rearrange("(a p) o -> p (a o)", p=P))

@@ -55,11 +55,7 @@ def tile_gather_matmul_kernel(tc, table, w, b, offs, out):
             flipped = flips.tile([P, BLOCKS * P], BF16, name="flipped")
             for a in range(BLOCKS):
                 nc.tensor.transpose(flipped[:, a * P : (a + 1) * P], rows[c][:, a, :], identity[:])
-            window_part = tokens[:, c * BLOCKS * P : (c + 1) * BLOCKS * P]
-            if c % 2 == 0:
-                nc.vector.tensor_copy(window_part, flipped[:])
-            else:
-                nc.scalar.copy(window_part, flipped[:])
+            nc.vector.tensor_copy(tokens[:, c * BLOCKS * P : (c + 1) * BLOCKS * P], flipped[:])
 
         for e in range(E):
             picked = tokens[:].indirect(offsets[:, e * (Q // 16) : (e + 1) * (Q // 16)])

@@ -10,6 +10,7 @@ Q = N // E
 CHUNKS = 4
 BLOCKS = S // P // CHUNKS
 OUT_BLOCKS = M // P
+DMA_ALIGN = 256
 
 FLOPS = 2 * K * M * N
 
@@ -24,21 +25,21 @@ def tile_gather_matmul_kernel(tc, table, w, b, offs, out):
     ):
 
         token_rows = table.rearrange("(c a p) k -> c p a k", c=CHUNKS, p=P)
-        rows = [held.tile([P, BLOCKS, K], BF16, name="rows%d" % c) for c in range(CHUNKS)]
+        rows = [held.tile([P, BLOCKS, K], BF16, name="rows%d" % c, align_bytes=DMA_ALIGN) for c in range(CHUNKS)]
         for c in range(CHUNKS):
             nc.sync.dma_start(rows[c][:], token_rows[c])
 
-        offsets = held.tile([P, N // 16], U16, name="offsets")
+        offsets = held.tile([P, N // 16], U16, name="offsets", align_bytes=DMA_ALIGN)
         nc.sync.dma_start(offsets[:], offs)
 
         features_first = w.rearrange("e k m -> k e m")
-        first_weights = held.tile([P, 1, M], BF16, name="first_weights")
+        first_weights = held.tile([P, 1, M], BF16, name="first_weights", align_bytes=DMA_ALIGN)
         nc.sync.dma_start(first_weights[:], features_first[:, :1, :])
 
         bias = held.tile([P, OUT_BLOCKS], F32, name="bias")
         nc.sync.dma_start(bias[:], b.rearrange("(a p) o -> p (a o)", p=P))
 
-        other_weights = held.tile([P, E - 1, M], BF16, name="other_weights")
+        other_weights = held.tile([P, E - 1, M], BF16, name="other_weights", align_bytes=DMA_ALIGN)
         nc.sync.dma_start(other_weights[:], features_first[:, 1:, :])
         weights = [first_weights[:, 0, :]] + [other_weights[:, e, :] for e in range(E - 1)]
 
@@ -62,6 +63,6 @@ def tile_gather_matmul_kernel(tc, table, w, b, offs, out):
             for a in range(OUT_BLOCKS):
                 product = products.tile([P, Q], F32, name="product")
                 nc.tensor.matmul(product[:], weights[e][:, a * P : (a + 1) * P], picked, start=True, stop=True)
-                result = results.tile([P, Q], F32, name="result")
+                result = results.tile([P, Q], F32, name="result", align_bytes=DMA_ALIGN)
                 nc.scalar.activation(result[:], product[:], GELU, bias=bias[:, a : a + 1])
                 nc.sync.dma_start(out[a * P : (a + 1) * P, e * Q : (e + 1) * Q], result[:])

import concourse.mybir as mybir
from concourse.masks import make_identity

BF16, F32, U16 = mybir.dt.bfloat16, mybir.dt.float32, mybir.dt.uint16
GELU = mybir.ActivationFunctionType.Gelu_apprx_tanh

P = 128
S, K, M, N, E = 1024, 128, 256, 2048, 4
Q = N // E
CHUNKS = 4
BLOCKS = S // P // CHUNKS
OUT_BLOCKS = M // P
DMA_ALIGN = 256

FLOPS = 2 * K * M * N


def tile_gather_matmul_kernel(tc, table, w, b, offs, out):
    nc = tc.nc
    with (
        tc.tile_pool(name="held", bufs=1) as held,
        tc.tile_pool(name="results", bufs=E * OUT_BLOCKS) as results,
        tc.psum_pool(name="flips", bufs=3) as flips,
        tc.psum_pool(name="products", bufs=4) as products,
    ):

        token_rows = table.rearrange("(c a p) k -> c p a k", c=CHUNKS, p=P)
        rows = [held.tile([P, BLOCKS, K], BF16, name="rows%d" % c, align_bytes=DMA_ALIGN) for c in range(CHUNKS)]
        for c in range(CHUNKS):
            nc.sync.dma_start(rows[c][:], token_rows[c])

        offsets = held.tile([P, N // 16], U16, name="offsets", align_bytes=DMA_ALIGN)
        nc.sync.dma_start(offsets[:], offs)

        features_first = w.rearrange("e k m -> k e m")
        first_weights = held.tile([P, 1, M], BF16, name="first_weights", align_bytes=DMA_ALIGN)
        nc.sync.dma_start(first_weights[:], features_first[:, :1, :])

        bias = held.tile([P, OUT_BLOCKS], F32, name="bias")
        nc.sync.dma_start(bias[:], b.rearrange("(a p) o -> p (a o)", p=P))

        other_weights = held.tile([P, E - 1, M], BF16, name="other_weights", align_bytes=DMA_ALIGN)
        nc.sync.dma_start(other_weights[:], features_first[:, 1:, :])
        weights = [first_weights[:, 0, :]] + [other_weights[:, e, :] for e in range(E - 1)]

        zero = held.tile([P, 1], F32, name="zero")
        nc.vector.memset(zero[:], 0.0)
        gelu_of_zero = held.tile([P, 1], F32, name="gelu_of_zero")
        nc.scalar.activation(gelu_of_zero[:], zero[:], GELU)

        identity = held.tile([P, P], BF16, name="identity")
        make_identity(nc, identity[:])

        tokens = held.tile([P, S], BF16, name="tokens")
        for c in range(CHUNKS):
            flipped = flips.tile([P, BLOCKS * P], BF16, name="flipped")
            for a in range(BLOCKS):
                nc.tensor.transpose(flipped[:, a * P : (a + 1) * P], rows[c][:, a, :], identity[:])
            nc.vector.tensor_copy(tokens[:, c * BLOCKS * P : (c + 1) * BLOCKS * P], flipped[:])

        for e in range(E):
            picked = tokens[:].indirect(offsets[:, e * (Q // 16) : (e + 1) * (Q // 16)])
            for a in range(OUT_BLOCKS):
                product = products.tile([P, Q], F32, name="product")
                nc.tensor.matmul(product[:], weights[e][:, a * P : (a + 1) * P], picked, start=True, stop=True)
                result = results.tile([P, Q], F32, name="result", align_bytes=DMA_ALIGN)
                nc.scalar.activation(result[:], product[:], GELU, bias=bias[:, a : a + 1])
                nc.sync.dma_start(out[a * P : (a + 1) * P, e * Q : (e + 1) * Q], result[:])
